import numpy as np
import ml_dtypes


def mxq(x, axis, fmt="e4m3"):
    dtype, down = {"e4m3": (ml_dtypes.float8_e4m3fn, 7), "e5m2": (ml_dtypes.float8_e5m2, 14)}[fmt]
    v = np.moveaxis(np.asarray(x, np.float32).astype(ml_dtypes.bfloat16).astype(np.float64), axis, -1)
    blocks = v.reshape(v.shape[:-1] + (-1, 32))
    amax = np.abs(blocks).max(-1, keepdims=True)
    byte = np.maximum(np.where(amax > 0, np.frexp(amax)[1] - 1 + 127, 0) - down, 1)
    scale = np.exp2(byte - 127.0)
    codes = (blocks / scale).astype(np.float32).astype(dtype).astype(np.float64)
    return np.moveaxis((codes * scale).reshape(v.shape), -1, axis)


WIDE = False


def mx_kscale(k):
    if not WIDE:
        return np.ones(k)
    levels = np.array([10, -10, 5, -5, 0])
    if k % 512:
        return np.exp2(np.random.permutation(np.resize(levels, k // 32))).repeat(32)
    a = np.empty((k // 512, 16))
    for p in range(k // 512):
        a[p, :8] = np.random.permutation(np.resize(levels, 8))
        for g in range(8):
            far = levels[np.abs(levels - a[p, g]) >= 10]
            a[p, g + 8] = far[np.random.randint(len(far))]
    return np.exp2(a.ravel()).repeat(32)


def f64(x):
    return np.asarray(x).astype(np.float64)


def striped(idx):
    return np.tile(idx.reshape(-1, 16).T, (8, 1)).astype(np.uint16)


def unstriped(offs):
    return offs[:16].T.reshape(-1).astype(np.int64)


def striped8(idx):
    return np.concatenate([x.reshape(-1, 16).T for x in idx]).astype(np.uint16)


def runs(offs, k):
    lists = np.stack([offs[16 * r : 16 * r + 16].T.reshape(-1) for r in range(8)]).astype(np.int64)
    return lists[np.arange(k) % 512 // 64]


def pack_weight(w):
    k, n = w.shape
    w = f64(np.asarray(w, np.float32).astype(ml_dtypes.bfloat16)).reshape(k // 32, 32, n)
    amax = np.abs(w).max(1)
    byte = np.clip(np.where(amax > 0, np.frexp(amax)[1] - 1 + 127 - 7, 1), 1, 254)
    scaled = (w * np.exp2(127.0 - byte)[:, None, :]).reshape(k, n).astype(np.float32)
    words = np.ascontiguousarray(scaled.reshape(k // 512, 128, 4, n).transpose(0, 1, 3, 2)).astype(ml_dtypes.float8_e4m3fn).view(np.uint8)
    return words, np.ascontiguousarray(byte.astype(np.uint8).reshape(k // 512, 16, n))


def unpack_weight(words, scales):
    g, p, n, _ = words.shape
    vals = np.ascontiguousarray(words).view(ml_dtypes.float8_e4m3fn).astype(np.float64) * np.repeat(np.exp2(scales.astype(np.float64) - 127.0), 8, axis=1)[..., None]
    return vals.transpose(0, 1, 3, 2).reshape(g * 512, n)


E2M1 = np.array([0.0, 0.5, 1.0, 1.5, 2.0, 3.0, 4.0, 6.0, -0.0, -0.5, -1.0, -1.5, -2.0, -3.0, -4.0, -6.0])


def pack_fp4(w):
    k, n = w.shape
    w = f64(np.asarray(w, np.float32).astype(ml_dtypes.bfloat16)).reshape(k // 32, 32, n)
    amax = np.abs(w).max(1)
    mant, ex = np.frexp(amax / 6.0)
    byte = np.clip(np.where(amax > 0, np.where(mant > 0.5, ex, ex - 1) + 127, 1), 1, 254)
    scaled = (w * np.exp2(127.0 - byte)[:, None, :]).reshape(k, n).astype(np.float32)
    c = np.ascontiguousarray(scaled.reshape(k // 512, 128, 4, n).transpose(0, 1, 3, 2)).astype(ml_dtypes.float4_e2m1fn).view(np.uint8) & 0xF
    words = (c[..., 0::2] | (c[..., 1::2] << 4)).reshape(k // 512, 128, 2 * n)
    return np.ascontiguousarray(words), np.ascontiguousarray(byte.astype(np.uint8).reshape(k // 512, 16, n))


def unpack_fp4(words, scales):
    g, _, n = scales.shape
    words = np.ascontiguousarray(words).reshape(g, 128, n, 2)
    nib = np.empty((g, 128, n, 4), np.uint8)
    nib[..., 0::2] = words & 0xF
    nib[..., 1::2] = words >> 4
    vals = E2M1[nib] * np.repeat(np.exp2(scales.astype(np.float64) - 127.0), 8, axis=1)[..., None]
    return vals.transpose(0, 1, 3, 2).reshape(g * 512, n)


def sigmoid(v):
    return 1.0 / (1.0 + np.exp(-np.maximum(v, -700.0)))

def planes(y):
    n, m = y.shape
    v = y.astype(np.float32).astype(ml_dtypes.bfloat16).astype(np.float64).reshape(n // 32, 32, m)
    top = np.abs(v).max(1)
    byte = np.clip(np.where(top > 0, np.frexp(top)[1] - 1 + 127 - 7, 1), 1, 254)
    codes = (v * np.exp2(127.0 - byte)[:, None, :]).reshape(n, m).astype(np.float32).astype(ml_dtypes.float8_e4m3fn).view(np.uint8)
    words = codes.reshape(n // 512, 128, 4, m).transpose(0, 1, 3, 2)
    return np.ascontiguousarray(words), np.ascontiguousarray(byte.astype(np.uint8).reshape(n // 512, 16, m))


K, T, S, N, H = 512, 2048, 512, 512, 512


def setup_inputs():
    n = np.random.standard_normal
    s = mx_kscale(K)[:, None]
    u = mx_kscale(H)
    packed_xT = pack_weight(n((K, T)) * s)
    packed_w1 = pack_fp4(n((K, H)) / np.sqrt(K) / s)
    packed_w2 = pack_fp4(n((K, H)) / np.sqrt(K) / s)
    packed_w3 = pack_fp4(n((H, N)) / np.sqrt(H) / u[:, None])
    return {
        "x_words": packed_xT[0],
        "x_scales": packed_xT[1],
        "w1_words": packed_w1[0],
        "w1_scales": packed_w1[1],
        "w2_words": packed_w2[0],
        "w2_scales": packed_w2[1],
        "gn": (np.random.uniform(0.5, 1.5, (H, 1)) * u[:, None]).astype(np.float32),
        "w3_words": packed_w3[0],
        "w3_scales": packed_w3[1],
        "offs": striped(np.random.permutation(T)[:S]),
        "two": striped(np.random.permutation(T)[:S]),
        "n1": striped8(np.stack([np.random.permutation(S) for _ in range(8)])),
        "n2": striped8(np.stack([np.random.permutation(S) for _ in range(8)])),
        "n3": striped8(np.stack([np.random.permutation(S) for _ in range(8)])),
    }


def reference(x_words, x_scales, w1_words, w1_scales, w2_words, w2_scales, gn, w3_words, w3_scales, offs, two, n1, n2, n3):
    xq = unpack_weight(x_words, x_scales)[:, unstriped(offs)]
    y = unpack_fp4(w1_words, w1_scales).T @ xq
    x_two = unpack_weight(x_words, x_scales)[:, unstriped(two)]
    d = unpack_fp4(w2_words, w2_scales).T @ x_two
    z = f64(gn) * (y + (sigmoid(d[np.arange(H)[:, None], runs(n2, H)] - d)) * (y[np.arange(H)[:, None], runs(n1, H)] - y))
    h = unpack_fp4(w3_words, w3_scales).T @ mxq(z, 0, "e4m3")
    st = h - (h[np.arange(N)[:, None], runs(n3, N)])
    out_0 = st - (0.5 * (st[np.arange(N)[:, None], runs(n3, N)]))
    return (out_0,) + planes(out_0)

@@ -1,0 +1,204 @@
+from contextlib import ExitStack
+
+import concourse.mybir as mybir
+
+F32 = mybir.dt.float32
+BF16 = mybir.dt.bfloat16
+I32 = mybir.dt.int32
+U32 = mybir.dt.uint32
+U16 = mybir.dt.uint16
+U8 = mybir.dt.uint8
+FP8X4 = mybir.dt.float8_e4m3fn_x4
+FP4X4 = mybir.dt.float4_e2m1fn_x4
+ALU = mybir.AluOpType
+ACT = mybir.ActivationFunctionType
+
+P = 128
+PACK = 4
+T = 2048
+S = 512
+FLOPS = 3 * 2 * 512 * 512 * 512
+
+
+def tile_picked_twlpullbtwice_none_po_kernel(
+    tc, x_words, x_scales, w1_words, w1_scales, w2_words, w2_scales, gn, w3_words, w3_scales,
+    offs, two, n1, n2, n3, out_0, out_1, out_2,
+):
+    nc = tc.nc
+    with ExitStack() as ctx:
+        keep = ctx.enter_context(tc.tile_pool(name="keep", bufs=1))
+        psum = ctx.enter_context(tc.psum_pool(name="psum", bufs=1))
+
+        def load_list(src, name):
+            tile = keep.tile([P, S // 16], U16, name=name)
+            nc.sync.dma_start(tile[:], src)
+            return tile
+
+        def load_scales(queue, tile, src):
+            for q in range(4):
+                queue.dma_start(tile[32 * q : 32 * q + 4, :].bitcast(I32), src[0, 4 * q : 4 * q + 4, :].bitcast(I32))
+
+        def scale_tile(width, name):
+            tile = keep.tile([P, width], U8, name=name, align_bytes=64)
+            nc.vector.memset(tile[:].bitcast(I32), 0)
+            return tile
+
+        xs = scale_tile(T, "xs")
+        w2s_raw = scale_tile(S, "w2s_raw")
+        w1s_raw = scale_tile(S, "w1s_raw")
+        w3s_raw = scale_tile(S, "w3s_raw")
+        warm_in = keep.tile([P, 1], F32, name="warm_in")
+        warm_out = keep.tile([P, 1], F32, name="warm_out")
+        nc.gpsimd.memset(warm_in[:], 0.0)
+        nc.scalar.activation(warm_out[:], warm_in[:], ACT.Sigmoid)
+
+        xw = keep.tile([P, T], U32, name="xw")
+        nc.sync.dma_start(xw[:].bitcast(I32), x_words[0].rearrange("p c r -> p (c r)").bitcast(I32))
+        load_scales(nc.sync, xs, x_scales)
+        two_t = load_list(two, "two_t")
+        offs_t = load_list(offs, "offs_t")
+
+        def load_words(queue, src, name):
+            tile = keep.tile([P, 2 * S], U8, name=name)
+            queue.dma_start(tile[:].bitcast(I32), src[0].bitcast(I32))
+            return tile
+
+        w2w_raw = load_words(nc.scalar, w2_words, "w2w_raw")
+        load_scales(nc.scalar, w2s_raw, w2_scales)
+        n2_t = load_list(n2, "n2_t")
+        w1w_raw = load_words(nc.scalar, w1_words, "w1w_raw")
+        load_scales(nc.scalar, w1s_raw, w1_scales)
+        n1_t = load_list(n1, "n1_t")
+        gain = keep.tile([P, PACK], F32, name="gain")
+        nc.gpsimd.dma_start(gain[:], gn.rearrange("(p t) o -> p (t o)", t=PACK))
+        w3w_raw = load_words(nc.gpsimd, w3_words, "w3w_raw")
+        load_scales(nc.gpsimd, w3s_raw, w3_scales)
+        n3_t = load_list(n3, "n3_t")
+
+        def deal(words_raw, scales_raw, name):
+            words = keep.tile([P, 2 * S], U8, name=name + "w", align_bytes=64)
+            scales = keep.tile([P, S], U8, name=name + "s", align_bytes=64)
+            nc.vector.tensor_copy(
+                words[:].rearrange("p (t m e) -> p m t e", t=PACK, e=2),
+                words_raw[:].rearrange("p (m t e) -> p m t e", t=PACK, e=2),
+            )
+            nc.vector.tensor_copy(
+                scales[:].rearrange("p (t m) -> p m t", t=PACK),
+                scales_raw[:].rearrange("p (m t) -> p m t", t=PACK),
+            )
+            return words, scales
+
+        def pick_scales(lst, name):
+            tile = keep.tile([P, S], U8, name=name, align_bytes=64)
+            nc.vector.tensor_copy(tile[:], xs[:].indirect(lst[:]))
+            return tile
+
+        def pick_words(lst, name):
+            tile = keep.tile([P, S], U32, name=name, align_bytes=64)
+            nc.vector.tensor_copy(tile[:], xw[:].indirect(lst[:]))
+            return tile
+
+        def product(bank, weights, t, words, scales):
+            w_words, w_scales = weights
+            nc.tensor.matmul_mx(
+                out=bank,
+                lhsT=w_words[:, 2 * P * t : 2 * P * (t + 1)].bitcast(FP4X4),
+                lhsT_scale=w_scales[:, P * t : P * (t + 1)],
+                rhs=words.bitcast(FP8X4),
+                rhs_scale=scales,
+                start=True,
+                stop=True,
+            )
+
+        def gather_sub(out, window, lst, lo, hi, other):
+            nc.vector.tensor_tensor(out, window[:].indirect(lst[:, lo // 16 : hi // 16]), other, ALU.subtract)
+
+        w2 = deal(w2w_raw, w2s_raw, "w2")
+        xs_two = pick_scales(two_t, "xs_two")
+        xs_off = pick_scales(offs_t, "xs_off")
+        xw_two = pick_words(two_t, "xw_two")
+        xw_off = pick_words(offs_t, "xw_off")
+        w1 = deal(w1w_raw, w1s_raw, "w1")
+
+        halves = [(0, 256), (256, 512)]
+        chunks = [(0, 256), (256, 384), (384, 512)]
+
+        d_bank = [psum.tile([P, S], F32, name="dh%d" % t) for t in range(PACK)]
+        y_bank = [psum.tile([P, S], F32, name="y%d" % t) for t in range(PACK)]
+        d_win = [keep.tile([P, S], F32, name="d_win%d" % t) for t in range(PACK)]
+        y_win = [keep.tile([P, S], F32, name="y_win%d" % t) for t in range(PACK)]
+        d_own = keep.tile([P, PACK, S], F32, name="d_own")
+        y_own = keep.tile([P, PACK, S], F32, name="y_own")
+        u = keep.tile([P, PACK, S], F32, name="u")
+        gate = keep.tile([P, PACK, S], F32, name="gate")
+        v = keep.tile([P, PACK, S], F32, name="v")
+        pull = keep.tile([P, PACK, S], F32, name="pull")
+
+        for t in range(PACK):
+            product(d_bank[t][:], w2, t, xw_two[:], xs_two[:])
+        for t in range(PACK):
+            product(y_bank[t][:], w1, t, xw_off[:], xs_off[:])
+        for t in range(PACK):
+            nc.scalar.copy(d_win[t][:], d_bank[t][:])
+            nc.scalar.copy(d_own[:, t, :], d_bank[t][:])
+        for t in range(PACK):
+            for lo, hi in halves:
+                gather_sub(u[:, t, lo:hi], d_win[t], n2_t, lo, hi, d_own[:, t, lo:hi])
+        for t in range(PACK):
+            nc.scalar.activation(y_win[t][:], y_bank[t][:], ACT.Copy, scale=gain[:, t : t + 1])
+            nc.scalar.activation(y_own[:, t, :], y_bank[t][:], ACT.Copy, scale=gain[:, t : t + 1])
+        for t in range(PACK):
+            nc.scalar.activation(gate[:, t, :], u[:, t, :], ACT.Sigmoid)
+        w3 = deal(w3w_raw, w3s_raw, "w3")
+
+        z_words = keep.tile([P, S], U32, name="z_words", align_bytes=64)
+        z_scales = keep.tile([P, S], U8, name="z_scales", align_bytes=64)
+        h_bank = [psum.tile([P, S], F32, name="dh%d" % t) for t in range(PACK)]
+        h_win = [keep.tile([P, S], F32, name="h_win%d" % t) for t in range(PACK)]
+        h_own = keep.tile([P, PACK, S], F32, name="h_own")
+
+        def by_four(ap):
+            return ap.rearrange("p t (c i) -> p c t i", i=4)
+
+        def woven(tile):
+            return tile[:].rearrange("p (c i t) -> p c t i", i=4, t=PACK)
+
+        for lo, hi in chunks:
+            for t in range(PACK):
+                gather_sub(v[:, t, lo:hi], y_win[t], n1_t, lo, hi, y_own[:, t, lo:hi])
+            nc.vector.tensor_tensor(pull[:, :, lo:hi], v[:, :, lo:hi], gate[:, :, lo:hi], ALU.mult)
+            z_bf = keep.tile([P, PACK * (hi - lo)], BF16, name="z_bf%d" % lo, align_bytes=64)
+            nc.vector.tensor_tensor(woven(z_bf), by_four(pull[:, :, lo:hi]), by_four(y_own[:, :, lo:hi]), ALU.add)
+            nc.vector.quantize_mx(out=z_words[:, lo:hi].bitcast(FP8X4), scales=z_scales[:, lo:hi], in_=z_bf[:])
+            for t in range(PACK):
+                product(h_bank[t][:, lo:hi], w3, t, z_words[:, lo:hi], z_scales[:, lo:hi])
+            for t in range(PACK):
+                nc.scalar.activation(h_win[t][:, lo:hi], h_bank[t][:, lo:hi], ACT.Copy, scale=0.5)
+                nc.scalar.activation(h_own[:, t, lo:hi], h_bank[t][:, lo:hi], ACT.Copy, scale=0.5)
+
+        m_win = [keep.tile([P, S], F32, name="m_win%d" % t) for t in range(PACK)]
+        m_own = keep.tile([P, PACK, S], F32, name="m_own")
+        for t in range(PACK):
+            for lo, hi in halves:
+                gather_sub(m_win[t][:, lo:hi], h_win[t], n3_t, lo, hi, h_own[:, t, lo:hi])
+            nc.scalar.activation(m_own[:, t, :], m_win[t][:], ACT.Copy, scale=2.0)
+
+        o_words = keep.tile([P, S], U32, name="o_words", align_bytes=64)
+        o_scales = keep.tile([P, S], U8, name="o_scales", align_bytes=64)
+        out_rows = out_0.rearrange("(p t) s -> p t s", t=PACK)
+        out_words = out_1[0].rearrange("p c r -> p (c r)").bitcast(I32)
+        for lo, hi in chunks:
+            res = keep.tile([P, PACK, hi - lo], F32, name="res%d" % lo)
+            for t in range(PACK):
+                gather_sub(res[:, t, :], m_win[t], n3_t, lo, hi, m_own[:, t, lo:hi])
+            nc.sync.dma_start(out_rows[:, :, lo:hi], res[:])
+            o_bf = keep.tile([P, PACK * (hi - lo)], BF16, name="o_bf%d" % lo, align_bytes=64)
+            if hi == S:
+                nc.vector.tensor_copy(woven(o_bf), by_four(res[:]))
+            else:
+                nc.scalar.copy(woven(o_bf), by_four(res[:]))
+            nc.vector.quantize_mx(out=o_words[:, lo:hi].bitcast(FP8X4), scales=o_scales[:, lo:hi], in_=o_bf[:])
+            nc.sync.dma_start(out_words[:, lo:hi], o_words[:, lo:hi].bitcast(I32))
+        for q in range(4):
+            queue = nc.scalar if q % 2 else nc.sync
+            queue.dma_start(out_2[0, 4 * q : 4 * q + 4, :].bitcast(I32), o_scales[32 * q : 32 * q + 4, :].bitcast(I32))

@@ -38,55 +38,57 @@ def tile_picked_twlpullbtwice_none_po_kernel(
             for q in range(4):
                 queue.dma_start(tile[32 * q : 32 * q + 4, :].bitcast(I32), src[0, 4 * q : 4 * q + 4, :].bitcast(I32))
 
-        def scale_tile(width, name):
+        def scale_tile(engine, width, name):
             tile = keep.tile([P, width], U8, name=name, align_bytes=64)
-            nc.vector.memset(tile[:].bitcast(I32), 0)
+            engine.memset(tile[:].bitcast(I32), 0)
             return tile
 
-        xs = scale_tile(T, "xs")
-        w2s_raw = scale_tile(S, "w2s_raw")
-        w1s_raw = scale_tile(S, "w1s_raw")
-        w3s_raw = scale_tile(S, "w3s_raw")
+        xs = scale_tile(nc.vector, T, "xs")
+        w2s_raw = scale_tile(nc.vector, S, "w2s_raw")
+        w1s_raw = scale_tile(nc.vector, S, "w1s_raw")
+        w3s_raw = scale_tile(nc.vector, S, "w3s_raw")
         warm_in = keep.tile([P, 1], F32, name="warm_in")
         warm_out = keep.tile([P, 1], F32, name="warm_out")
-        nc.gpsimd.memset(warm_in[:], 0.0)
+        nc.vector.memset(warm_in[:], 0.0)
         nc.scalar.activation(warm_out[:], warm_in[:], ACT.Sigmoid)
-
-        xw = keep.tile([P, T], U32, name="xw")
-        nc.sync.dma_start(xw[:].bitcast(I32), x_words[0].rearrange("p c r -> p (c r)").bitcast(I32))
-        load_scales(nc.sync, xs, x_scales)
-        two_t = load_list(two, "two_t")
-        offs_t = load_list(offs, "offs_t")
 
         def load_words(queue, src, name):
             tile = keep.tile([P, 2 * S], U8, name=name)
             queue.dma_start(tile[:].bitcast(I32), src[0].bitcast(I32))
             return tile
 
-        w2w_raw = load_words(nc.scalar, w2_words, "w2w_raw")
-        load_scales(nc.scalar, w2s_raw, w2_scales)
+        w2w_raw = load_words(nc.sync, w2_words, "w2w_raw")
+        two_t = load_list(two, "two_t")
+        xw = keep.tile([P, T], U32, name="xw")
+        nc.sync.dma_start(xw[:].bitcast(I32), x_words[0].rearrange("p c r -> p (c r)").bitcast(I32))
+        w1w_raw = load_words(nc.sync, w1_words, "w1w_raw")
+        load_scales(nc.sync, xs, x_scales)
+        load_scales(nc.sync, w2s_raw, w2_scales)
+        offs_t = load_list(offs, "offs_t")
+        w3w_raw = load_words(nc.sync, w3_words, "w3w_raw")
         n2_t = load_list(n2, "n2_t")
-        w1w_raw = load_words(nc.scalar, w1_words, "w1w_raw")
-        load_scales(nc.scalar, w1s_raw, w1_scales)
         n1_t = load_list(n1, "n1_t")
+        n3_t = load_list(n3, "n3_t")
+        load_scales(nc.gpsimd, w1s_raw, w1_scales)
         gain = keep.tile([P, PACK], F32, name="gain")
         nc.gpsimd.dma_start(gain[:], gn.rearrange("(p t) o -> p (t o)", t=PACK))
-        w3w_raw = load_words(nc.gpsimd, w3_words, "w3w_raw")
         load_scales(nc.gpsimd, w3s_raw, w3_scales)
-        n3_t = load_list(n3, "n3_t")
 
-        def deal(words_raw, scales_raw, name):
-            words = keep.tile([P, 2 * S], U8, name=name + "w", align_bytes=64)
-            scales = keep.tile([P, S], U8, name=name + "s", align_bytes=64)
+        def deal_words(words_raw, name):
+            words = keep.tile([P, 2 * S], U8, name=name, align_bytes=64)
             nc.vector.tensor_copy(
-                words[:].rearrange("p (t m e) -> p m t e", t=PACK, e=2),
-                words_raw[:].rearrange("p (m t e) -> p m t e", t=PACK, e=2),
+                words[:].rearrange("p (t m e) -> p t m e", t=PACK, e=2),
+                words_raw[:].rearrange("p (m t e) -> p t m e", t=PACK, e=2),
             )
+            return words
+
+        def deal_scales(scales_raw, name):
+            scales = keep.tile([P, S], U8, name=name, align_bytes=64)
             nc.vector.tensor_copy(
-                scales[:].rearrange("p (t m) -> p m t", t=PACK),
-                scales_raw[:].rearrange("p (m t) -> p m t", t=PACK),
+                scales[:].rearrange("p (t m) -> p t m", t=PACK),
+                scales_raw[:].rearrange("p (m t) -> p t m", t=PACK),
             )
-            return words, scales
+            return scales
 
         def pick_scales(lst, name):
             tile = keep.tile([P, S], U8, name=name, align_bytes=64)
@@ -113,12 +115,15 @@ def tile_picked_twlpullbtwice_none_po_kernel(
         def gather_sub(out, window, lst, lo, hi, other):
             nc.vector.tensor_tensor(out, window[:].indirect(lst[:, lo // 16 : hi // 16]), other, ALU.subtract)
 
-        w2 = deal(w2w_raw, w2s_raw, "w2")
+        w2w = deal_words(w2w_raw, "w2w")
+        w1w = deal_words(w1w_raw, "w1w")
+        w3w = deal_words(w3w_raw, "w3w")
+        w2 = (w2w, deal_scales(w2s_raw, "w2s"))
         xs_two = pick_scales(two_t, "xs_two")
-        xs_off = pick_scales(offs_t, "xs_off")
         xw_two = pick_words(two_t, "xw_two")
+        xs_off = pick_scales(offs_t, "xs_off")
         xw_off = pick_words(offs_t, "xw_off")
-        w1 = deal(w1w_raw, w1s_raw, "w1")
+        w1 = (w1w, deal_scales(w1s_raw, "w1s"))
 
         halves = [(0, 256), (256, 512)]
         chunks = [(0, 256), (256, 384), (384, 512)]
@@ -149,7 +154,7 @@ def tile_picked_twlpullbtwice_none_po_kernel(
             nc.scalar.activation(y_own[:, t, :], y_bank[t][:], ACT.Copy, scale=gain[:, t : t + 1])
         for t in range(PACK):
             nc.scalar.activation(gate[:, t, :], u[:, t, :], ACT.Sigmoid)
-        w3 = deal(w3w_raw, w3s_raw, "w3")
+        w3 = (w3w, deal_scales(w3s_raw, "w2s"))
 
         z_words = keep.tile([P, S], U32, name="z_words", align_bytes=64)
         z_scales = keep.tile([P, S], U8, name="z_scales", align_bytes=64)
@@ -166,14 +171,20 @@ def tile_picked_twlpullbtwice_none_po_kernel(
         for lo, hi in chunks:
             for t in range(PACK):
                 gather_sub(v[:, t, lo:hi], y_win[t], n1_t, lo, hi, y_own[:, t, lo:hi])
-            nc.vector.tensor_tensor(pull[:, :, lo:hi], v[:, :, lo:hi], gate[:, :, lo:hi], ALU.mult)
-            z_bf = keep.tile([P, PACK * (hi - lo)], BF16, name="z_bf%d" % lo, align_bytes=64)
-            nc.vector.tensor_tensor(woven(z_bf), by_four(pull[:, :, lo:hi]), by_four(y_own[:, :, lo:hi]), ALU.add)
-            nc.vector.quantize_mx(out=z_words[:, lo:hi].bitcast(FP8X4), scales=z_scales[:, lo:hi], in_=z_bf[:])
+            mid = (lo + hi) // 2
+            parts = [(lo, mid), (mid, hi)] if hi == S else [(lo, hi)]
+            z_bf = [keep.tile([P, PACK * (b - a)], BF16, name="z_bf%d" % a, align_bytes=64) for a, b in parts]
+            for a, b in parts:
+                nc.vector.tensor_tensor(pull[:, :, a:b], v[:, :, a:b], gate[:, :, a:b], ALU.mult)
+            for i, (a, b) in enumerate(parts):
+                nc.vector.tensor_tensor(woven(z_bf[i]), by_four(pull[:, :, a:b]), by_four(y_own[:, :, a:b]), ALU.add)
+            for i, (a, b) in enumerate(parts):
+                nc.vector.quantize_mx(out=z_words[:, a:b].bitcast(FP8X4), scales=z_scales[:, a:b], in_=z_bf[i][:])
             for t in range(PACK):
                 product(h_bank[t][:, lo:hi], w3, t, z_words[:, lo:hi], z_scales[:, lo:hi])
             for t in range(PACK):
                 nc.scalar.activation(h_win[t][:, lo:hi], h_bank[t][:, lo:hi], ACT.Copy, scale=0.5)
+            for t in range(PACK):
                 nc.scalar.activation(h_own[:, t, lo:hi], h_bank[t][:, lo:hi], ACT.Copy, scale=0.5)
 
         m_win = [keep.tile([P, S], F32, name="m_win%d" % t) for t in range(PACK)]

@@ -1,6 +1,7 @@
 from contextlib import ExitStack
 
 import concourse.mybir as mybir
+from concourse.masks import make_identity
 
 F32 = mybir.dt.float32
 BF16 = mybir.dt.bfloat16
@@ -53,50 +54,52 @@ def tile_picked_twlpullbtwice_none_po_kernel(
         nc.scalar.activation(warm_out[:], warm_in[:], ACT.Sigmoid)
 
         def load_words(queue, src, name):
-            tile = keep.tile([P, 2 * S], U8, name=name)
+            tile = keep.tile([P, 2 * S], U8, name=name, align_bytes=64)
             queue.dma_start(tile[:].bitcast(I32), src[0].bitcast(I32))
             return tile
 
         w2w_raw = load_words(nc.sync, w2_words, "w2w_raw")
         two_t = load_list(two, "two_t")
-        xw = keep.tile([P, T], U32, name="xw")
-        nc.sync.dma_start(xw[:].bitcast(I32), x_words[0].rearrange("p c r -> p (c r)").bitcast(I32))
-        w1w_raw = load_words(nc.sync, w1_words, "w1w_raw")
-        load_scales(nc.sync, xs, x_scales)
-        load_scales(nc.sync, w2s_raw, w2_scales)
         offs_t = load_list(offs, "offs_t")
-        w3w_raw = load_words(nc.sync, w3_words, "w3w_raw")
+        load_scales(nc.sync, xs, x_scales)
+        xw = keep.tile([P, T], U32, name="xw", align_bytes=64)
+        nc.sync.dma_start(xw[:].bitcast(I32), x_words[0].rearrange("p c r -> p (c r)").bitcast(I32))
+        load_scales(nc.sync, w2s_raw, w2_scales)
+        w1w_raw = load_words(nc.sync, w1_words, "w1w_raw")
         n2_t = load_list(n2, "n2_t")
-        n1_t = load_list(n1, "n1_t")
-        n3_t = load_list(n3, "n3_t")
-        load_scales(nc.gpsimd, w1s_raw, w1_scales)
+        load_scales(nc.sync, w1s_raw, w1_scales)
         gain = keep.tile([P, PACK], F32, name="gain")
-        nc.gpsimd.dma_start(gain[:], gn.rearrange("(p t) o -> p (t o)", t=PACK))
-        load_scales(nc.gpsimd, w3s_raw, w3_scales)
+        nc.sync.dma_start(gain[:], gn.rearrange("(p t) o -> p (t o)", t=PACK))
+        n1_t = load_list(n1, "n1_t")
+        w3w_raw = load_words(nc.sync, w3_words, "w3w_raw")
+        load_scales(nc.sync, w3s_raw, w3_scales)
+        n3_t = load_list(n3, "n3_t")
+        ident = keep.tile([P, P], F32, name="ident")
+        make_identity(nc, ident[:])
 
-        def deal_words(words_raw, name):
-            words = keep.tile([P, 2 * S], U8, name=name, align_bytes=64)
+        def deal_words(words_raw, name, tag):
+            words = keep.tile([P, 2 * S], U8, name=name, tag=tag, align_bytes=64)
             nc.vector.tensor_copy(
                 words[:].rearrange("p (t m e) -> p t m e", t=PACK, e=2),
                 words_raw[:].rearrange("p (m t e) -> p t m e", t=PACK, e=2),
             )
             return words
 
-        def deal_scales(scales_raw, name):
-            scales = keep.tile([P, S], U8, name=name, align_bytes=64)
+        def deal_scales(scales_raw, name, tag):
+            scales = keep.tile([P, S], U8, name=name, tag=tag, align_bytes=64)
             nc.vector.tensor_copy(
                 scales[:].rearrange("p (t m) -> p t m", t=PACK),
                 scales_raw[:].rearrange("p (m t) -> p t m", t=PACK),
             )
             return scales
 
-        def pick_scales(lst, name):
-            tile = keep.tile([P, S], U8, name=name, align_bytes=64)
+        def pick_scales(lst, name, tag):
+            tile = keep.tile([P, S], U8, name=name, tag=tag, align_bytes=64)
             nc.vector.tensor_copy(tile[:], xs[:].indirect(lst[:]))
             return tile
 
-        def pick_words(lst, name):
-            tile = keep.tile([P, S], U32, name=name, align_bytes=64)
+        def pick_words(lst, name, tag):
+            tile = keep.tile([P, S], U32, name=name, tag=tag, align_bytes=64)
             nc.vector.tensor_copy(tile[:], xw[:].indirect(lst[:]))
             return tile
 
@@ -115,52 +118,16 @@ def tile_picked_twlpullbtwice_none_po_kernel(
         def gather_sub(out, window, lst, lo, hi, other):
             nc.vector.tensor_tensor(out, window[:].indirect(lst[:, lo // 16 : hi // 16]), other, ALU.subtract)
 
-        w2w = deal_words(w2w_raw, "w2w")
-        w1w = deal_words(w1w_raw, "w1w")
-        w3w = deal_words(w3w_raw, "w3w")
-        w2 = (w2w, deal_scales(w2s_raw, "w2s"))
-        xs_two = pick_scales(two_t, "xs_two")
-        xw_two = pick_words(two_t, "xw_two")
-        xs_off = pick_scales(offs_t, "xs_off")
-        xw_off = pick_words(offs_t, "xw_off")
-        w1 = (w1w, deal_scales(w1s_raw, "w1s"))
+        w2w = deal_words(w2w_raw, "w2w", "w2w")
+        xs_two = pick_scales(two_t, "xs_two", "xs_two")
+        xs_off = pick_scales(offs_t, "xs_off", "xs_off")
+        xw_two = pick_words(two_t, "xw_two", "xw_two")
+        w2 = (w2w, deal_scales(w2s_raw, "w2s", "w2s"))
+        xw_off = pick_words(offs_t, "xw_off", "w2s_raw")
+        w1 = (deal_words(w1w_raw, "w1w", "xw"), deal_scales(w1s_raw, "w1s", "w1w_raw"))
 
-        halves = [(0, 256), (256, 512)]
-        chunks = [(0, 256), (256, 384), (384, 512)]
-
-        d_bank = [psum.tile([P, S], F32, name="dh%d" % t) for t in range(PACK)]
-        y_bank = [psum.tile([P, S], F32, name="y%d" % t) for t in range(PACK)]
-        d_win = [keep.tile([P, S], F32, name="d_win%d" % t) for t in range(PACK)]
-        y_win = [keep.tile([P, S], F32, name="y_win%d" % t) for t in range(PACK)]
-        d_own = keep.tile([P, PACK, S], F32, name="d_own")
-        y_own = keep.tile([P, PACK, S], F32, name="y_own")
-        u = keep.tile([P, PACK, S], F32, name="u")
-        gate = keep.tile([P, PACK, S], F32, name="gate")
-        v = keep.tile([P, PACK, S], F32, name="v")
-        pull = keep.tile([P, PACK, S], F32, name="pull")
-
-        for t in range(PACK):
-            product(d_bank[t][:], w2, t, xw_two[:], xs_two[:])
-        for t in range(PACK):
-            product(y_bank[t][:], w1, t, xw_off[:], xs_off[:])
-        for t in range(PACK):
-            nc.scalar.copy(d_win[t][:], d_bank[t][:])
-            nc.scalar.copy(d_own[:, t, :], d_bank[t][:])
-        for t in range(PACK):
-            for lo, hi in halves:
-                gather_sub(u[:, t, lo:hi], d_win[t], n2_t, lo, hi, d_own[:, t, lo:hi])
-        for t in range(PACK):
-            nc.scalar.activation(y_win[t][:], y_bank[t][:], ACT.Copy, scale=gain[:, t : t + 1])
-            nc.scalar.activation(y_own[:, t, :], y_bank[t][:], ACT.Copy, scale=gain[:, t : t + 1])
-        for t in range(PACK):
-            nc.scalar.activation(gate[:, t, :], u[:, t, :], ACT.Sigmoid)
-        w3 = (w3w, deal_scales(w3s_raw, "w2s"))
-
-        z_words = keep.tile([P, S], U32, name="z_words", align_bytes=64)
-        z_scales = keep.tile([P, S], U8, name="z_scales", align_bytes=64)
-        h_bank = [psum.tile([P, S], F32, name="dh%d" % t) for t in range(PACK)]
-        h_win = [keep.tile([P, S], F32, name="h_win%d" % t) for t in range(PACK)]
-        h_own = keep.tile([P, PACK, S], F32, name="h_own")
+        last = PACK - 1
+        pieces = [(0, 256), (256, 384), (384, 512)]
 
         def by_four(ap):
             return ap.rearrange("p t (c i) -> p c t i", i=4)
@@ -168,47 +135,110 @@ def tile_picked_twlpullbtwice_none_po_kernel(
         def woven(tile):
             return tile[:].rearrange("p (c i t) -> p c t i", i=4, t=PACK)
 
-        for lo, hi in chunks:
-            for t in range(PACK):
-                gather_sub(v[:, t, lo:hi], y_win[t], n1_t, lo, hi, y_own[:, t, lo:hi])
-            mid = (lo + hi) // 2
-            parts = [(lo, mid), (mid, hi)] if hi == S else [(lo, hi)]
-            z_bf = [keep.tile([P, PACK * (b - a)], BF16, name="z_bf%d" % a, align_bytes=64) for a, b in parts]
-            for a, b in parts:
-                nc.vector.tensor_tensor(pull[:, :, a:b], v[:, :, a:b], gate[:, :, a:b], ALU.mult)
-            for i, (a, b) in enumerate(parts):
-                nc.vector.tensor_tensor(woven(z_bf[i]), by_four(pull[:, :, a:b]), by_four(y_own[:, :, a:b]), ALU.add)
-            for i, (a, b) in enumerate(parts):
-                nc.vector.quantize_mx(out=z_words[:, a:b].bitcast(FP8X4), scales=z_scales[:, a:b], in_=z_bf[i][:])
-            for t in range(PACK):
-                product(h_bank[t][:, lo:hi], w3, t, z_words[:, lo:hi], z_scales[:, lo:hi])
-            for t in range(PACK):
-                nc.scalar.activation(h_win[t][:, lo:hi], h_bank[t][:, lo:hi], ACT.Copy, scale=0.5)
-            for t in range(PACK):
-                nc.scalar.activation(h_own[:, t, lo:hi], h_bank[t][:, lo:hi], ACT.Copy, scale=0.5)
+        halves = [(0, 256), (256, 512)]
+        d_bank = [psum.tile([P, S], F32, name="bank%d" % t) for t in range(PACK)]
+        y_bank = [psum.tile([P, S], F32, name="bank%d" % (PACK + t)) for t in range(PACK)]
+        d_win = [keep.tile([P, S], F32, name="d_win%d" % t) for t in range(PACK)]
+        y_win = [keep.tile([P, S], F32, name="y_win%d" % t) for t in range(PACK)]
+        h_win = [keep.tile([P, 2 * S], F32, name="h_win%d" % t) for t in range(PACK)]
+        m_win = [keep.tile([P, 2 * S if t < last else S], F32, name="m_win%d" % t) for t in range(PACK)]
+        gate_last = keep.tile([P, S], F32, name="gate_last")
+        u = [h_win[t][:, S:] for t in range(PACK)]
+        gate_t = [m_win[t][:, S:] for t in range(last)] + [gate_last[:]]
+        y_own = keep.tile([P, PACK, S], F32, name="y_own")
+        v = keep.tile([P, PACK, S], F32, name="v")
+        pull = keep.tile([P, PACK, S], F32, name="pull")
 
-        m_win = [keep.tile([P, S], F32, name="m_win%d" % t) for t in range(PACK)]
-        m_own = keep.tile([P, PACK, S], F32, name="m_own")
+        for t in range(PACK):
+            product(d_bank[t][:], w2, t, xw_two[:], xs_two[:])
+        w3 = (deal_words(w3w_raw, "w3w", "w2w"), deal_scales(w3s_raw, "w3s", "w2s"))
+        for t in range(PACK):
+            product(y_bank[t][:], w1, t, xw_off[:], xs_off[:])
+        for t in range(PACK):
+            nc.scalar.copy(d_win[t][:], d_bank[t][:])
         for t in range(PACK):
             for lo, hi in halves:
+                picked = d_win[t][:].indirect(n2_t[:, lo // 16 : hi // 16])
+                nc.vector.tensor_scalar(u[t][:, lo:hi], picked, -1.0, 0.0, ALU.mult, ALU.add)
+        for t in range(PACK):
+            nc.scalar.activation(y_win[t][:], y_bank[t][:], ACT.Copy, scale=gain[:, t : t + 1])
+            nc.scalar.activation(y_own[:, t, :], y_bank[t][:], ACT.Copy, scale=gain[:, t : t + 1])
+
+        def turn(out, term, start, stop):
+            nc.tensor.matmul(out, term, ident[:], start=start, stop=stop, is_transpose=True)
+
+        blocks = [slice(b * P, (b + 1) * P) for b in range(S // P)]
+        for t in range(PACK):
+            diff = psum.tile([P, S], F32, name="bank%d" % t)
+            for b, cols in enumerate(blocks):
+                turn(diff[:, cols], d_win[t][:, cols], b == 0, False)
+            for b, cols in enumerate(blocks):
+                turn(diff[:, cols], u[t][:, cols], False, b == len(blocks) - 1)
+            nc.scalar.activation(gate_t[t], diff[:], ACT.Sigmoid, scale=-1.0)
+        gate = {}
+        for h in range(2):
+            for j in range(2):
+                gate[h, j] = psum.tile([P, 2, 256], F32, name="bank%d" % (PACK + 2 * j + h))
+        for t in range(PACK):
+            for b, cols in enumerate(blocks):
+                turn(gate[b // 2, t // 2][:, t % 2, blocks[b % 2]], gate_t[t][:, cols], True, True)
+
+        z_words = keep.tile([P, S], U32, name="z_words", align_bytes=64)
+        z_scales = keep.tile([P, S], U8, name="z_scales", align_bytes=64)
+        h_own = keep.tile([P, PACK, S], F32, name="h_own")
+        groups = [((0, 2), (2, 4)), ((0, 4),), ((0, 1), (1, 4))]
+        h_parts = []
+        for h, (a, b) in enumerate(halves):
+            for t in range(PACK):
+                gather_sub(v[:, t, a:b], y_win[t], n1_t, a, b, y_own[:, t, a:b])
+            for j in range(2):
+                pair = slice(2 * j, 2 * j + 2)
+                nc.vector.tensor_tensor(pull[:, pair, a:b], gate[h, j][:], v[:, pair, a:b], ALU.mult)
+            for (lo, hi), spans in zip(pieces, groups):
+                if a <= lo < b:
+                    z_bf = keep.tile([P, PACK * (hi - lo)], BF16, name="z_bf%d" % lo, align_bytes=64)
+                    nc.vector.tensor_tensor(woven(z_bf), by_four(pull[:, :, lo:hi]), by_four(y_own[:, :, lo:hi]), ALU.add)
+                    nc.vector.quantize_mx(out=z_words[:, lo:hi].bitcast(FP8X4), scales=z_scales[:, lo:hi], in_=z_bf[:])
+                    for t0, t1 in spans:
+                        bank = psum.tile([P, t1 - t0, hi - lo], F32, name="bank%d" % len(h_parts))
+                        for t in range(t0, t1):
+                            product(bank[:, t - t0, :], w3, t, z_words[:, lo:hi], z_scales[:, lo:hi])
+                        h_parts.append((bank, t0, t1, lo, hi))
+        for t in range(PACK):
+            for bank, t0, t1, lo, hi in h_parts:
+                if t0 <= t < t1:
+                    nc.scalar.activation(h_win[t][:, lo:hi], bank[:, t - t0, :], ACT.Copy, scale=0.5)
+            for bank, t0, t1, lo, hi in h_parts:
+                if t0 == t:
+                    nc.scalar.activation(h_own[:, t0:t1, lo:hi], bank[:], ACT.Copy, scale=0.5)
+
+        m_own = keep.tile([P, PACK, S], F32, name="m_own")
+        for t in range(PACK):
+            for lo, hi in ((0, 256), (256, 512)) if t == 0 else ((0, 512),):
                 gather_sub(m_win[t][:, lo:hi], h_win[t], n3_t, lo, hi, h_own[:, t, lo:hi])
-            nc.scalar.activation(m_own[:, t, :], m_win[t][:], ACT.Copy, scale=2.0)
+            nc.scalar.activation(m_own[:, t, :], m_win[t][:, :S], ACT.Copy, scale=2.0)
 
         o_words = keep.tile([P, S], U32, name="o_words", align_bytes=64)
         o_scales = keep.tile([P, S], U8, name="o_scales", align_bytes=64)
         out_rows = out_0.rearrange("(p t) s -> p t s", t=PACK)
         out_words = out_1[0].rearrange("p c r -> p (c r)").bitcast(I32)
-        for lo, hi in chunks:
-            res = keep.tile([P, PACK, hi - lo], F32, name="res%d" % lo)
-            for t in range(PACK):
-                gather_sub(res[:, t, :], m_win[t], n3_t, lo, hi, m_own[:, t, lo:hi])
-            nc.sync.dma_start(out_rows[:, :, lo:hi], res[:])
-            o_bf = keep.tile([P, PACK * (hi - lo)], BF16, name="o_bf%d" % lo, align_bytes=64)
-            if hi == S:
-                nc.vector.tensor_copy(woven(o_bf), by_four(res[:]))
+        res = keep.tile([P, PACK, S], F32, name="res")
+        for t in range(last):
+            gather_sub(res[:, t, :], m_win[t], n3_t, 0, S, m_own[:, t, :])
+            nc.sync.dma_start(out_rows[:, t, :], res[:, t, :])
+        for lo, hi in pieces:
+            gather_sub(res[:, last, lo:hi], m_win[last], n3_t, lo, hi, m_own[:, last, lo:hi])
+        nc.sync.dma_start(out_rows[:, last, :], res[:, last, :])
+        o_bf = [keep.tile([P, PACK * (hi - lo)], BF16, name="o_bf%d" % lo, align_bytes=64) for lo, hi in pieces]
+        for i, (lo, hi) in enumerate(pieces):
+            if i == 0:
+                nc.scalar.copy(woven(o_bf[i]), by_four(res[:, :, lo:hi]))
             else:
-                nc.scalar.copy(woven(o_bf), by_four(res[:]))
-            nc.vector.quantize_mx(out=o_words[:, lo:hi].bitcast(FP8X4), scales=o_scales[:, lo:hi], in_=o_bf[:])
+                nc.vector.tensor_copy(woven(o_bf[i]), by_four(res[:, :, lo:hi]))
+        for i in (1, 2, 0):
+            lo, hi = pieces[i]
+            nc.vector.quantize_mx(out=o_words[:, lo:hi].bitcast(FP8X4), scales=o_scales[:, lo:hi], in_=o_bf[i][:])
+        for lo, hi in ((256, 512), (0, 256)):
             nc.sync.dma_start(out_words[:, lo:hi], o_words[:, lo:hi].bitcast(I32))
         for q in range(4):
             queue = nc.scalar if q % 2 else nc.sync

@@ -15,10 +15,15 @@ ALU = mybir.AluOpType
 ACT = mybir.ActivationFunctionType
 
 P = 128
-PACK = 4
+SLABS = 4
 T = 2048
 S = 512
-FLOPS = 3 * 2 * 512 * 512 * 512
+GROUP = 16
+FLOPS = 3 * 2 * S * S * S
+
+HALVES = ((0, S // 2), (S // 2, S))
+PIECES = ((0, S // 2), (S // 2, 3 * S // 4), (3 * S // 4, S))
+H_BANK_SLABS = (((0, 2), (2, 4)), ((0, 4),), ((0, 1), (1, 4)))
 
 
 def tile_picked_twlpullbtwice_none_po_kernel(
@@ -26,220 +31,223 @@ def tile_picked_twlpullbtwice_none_po_kernel(
     offs, two, n1, n2, n3, out_0, out_1, out_2,
 ):
     nc = tc.nc
+    last = SLABS - 1
     with ExitStack() as ctx:
         keep = ctx.enter_context(tc.tile_pool(name="keep", bufs=1))
         psum = ctx.enter_context(tc.psum_pool(name="psum", bufs=1))
 
+        def bank(number, shape):
+            return psum.tile(shape, F32, name="bank%d" % number)
+
+        def scale_tile(width, name):
+            tile = keep.tile([P, width], U8, name=name, align_bytes=64)
+            nc.vector.memset(tile[:].bitcast(I32), 0)
+            return tile
+
+        def load_scales(tile, src):
+            for q in range(4):
+                nc.sync.dma_start(tile[32 * q : 32 * q + 4, :].bitcast(I32), src[0, 4 * q : 4 * q + 4, :].bitcast(I32))
+
         def load_list(src, name):
-            tile = keep.tile([P, S // 16], U16, name=name)
+            tile = keep.tile([P, S // GROUP], U16, name=name)
             nc.sync.dma_start(tile[:], src)
             return tile
 
-        def load_scales(queue, tile, src):
-            for q in range(4):
-                queue.dma_start(tile[32 * q : 32 * q + 4, :].bitcast(I32), src[0, 4 * q : 4 * q + 4, :].bitcast(I32))
-
-        def scale_tile(engine, width, name):
-            tile = keep.tile([P, width], U8, name=name, align_bytes=64)
-            engine.memset(tile[:].bitcast(I32), 0)
-            return tile
-
-        xs = scale_tile(nc.vector, T, "xs")
-        w2s_raw = scale_tile(nc.vector, S, "w2s_raw")
-        w1s_raw = scale_tile(nc.vector, S, "w1s_raw")
-        w3s_raw = scale_tile(nc.vector, S, "w3s_raw")
-        warm_in = keep.tile([P, 1], F32, name="warm_in")
-        warm_out = keep.tile([P, 1], F32, name="warm_out")
-        nc.vector.memset(warm_in[:], 0.0)
-        nc.scalar.activation(warm_out[:], warm_in[:], ACT.Sigmoid)
-
-        def load_words(queue, src, name):
+        def load_weight_words(src, name):
             tile = keep.tile([P, 2 * S], U8, name=name, align_bytes=64)
-            queue.dma_start(tile[:].bitcast(I32), src[0].bitcast(I32))
+            nc.sync.dma_start(tile[:].bitcast(I32), src[0].bitcast(I32))
             return tile
 
-        w2w_raw = load_words(nc.sync, w2_words, "w2w_raw")
-        two_t = load_list(two, "two_t")
-        offs_t = load_list(offs, "offs_t")
-        load_scales(nc.sync, xs, x_scales)
-        xw = keep.tile([P, T], U32, name="xw", align_bytes=64)
-        nc.sync.dma_start(xw[:].bitcast(I32), x_words[0].rearrange("p c r -> p (c r)").bitcast(I32))
-        load_scales(nc.sync, w2s_raw, w2_scales)
-        w1w_raw = load_words(nc.sync, w1_words, "w1w_raw")
-        n2_t = load_list(n2, "n2_t")
-        load_scales(nc.sync, w1s_raw, w1_scales)
-        gain = keep.tile([P, PACK], F32, name="gain")
-        nc.sync.dma_start(gain[:], gn.rearrange("(p t) o -> p (t o)", t=PACK))
-        n1_t = load_list(n1, "n1_t")
-        w3w_raw = load_words(nc.sync, w3_words, "w3w_raw")
-        load_scales(nc.sync, w3s_raw, w3_scales)
-        n3_t = load_list(n3, "n3_t")
+        x_scale_table = scale_tile(T, "x_scale_table")
+        w2_scales_raw = scale_tile(S, "w2_scales_raw")
+        w1_scales_raw = scale_tile(S, "w1_scales_raw")
+        w3_scales_raw = scale_tile(S, "w3_scales_raw")
         ident = keep.tile([P, P], F32, name="ident")
-        make_identity(nc, ident[:])
+        nc.vector.memset(ident[:], 0.0)
+        make_identity(nc, ident[:], nomemset=True)
 
-        def deal_words(words_raw, name, tag):
-            words = keep.tile([P, 2 * S], U8, name=name, tag=tag, align_bytes=64)
-            nc.vector.tensor_copy(
-                words[:].rearrange("p (t m e) -> p t m e", t=PACK, e=2),
-                words_raw[:].rearrange("p (m t e) -> p t m e", t=PACK, e=2),
+        w2_words_raw = load_weight_words(w2_words, "w2_words_raw")
+        two_list = load_list(two, "two_list")
+        offs_list = load_list(offs, "offs_list")
+        load_scales(x_scale_table, x_scales)
+        x_word_table = keep.tile([P, T], U32, name="x_word_table", align_bytes=64)
+        nc.sync.dma_start(x_word_table[:].bitcast(I32), x_words[0].rearrange("p c r -> p (c r)").bitcast(I32))
+        load_scales(w2_scales_raw, w2_scales)
+        w1_words_raw = load_weight_words(w1_words, "w1_words_raw")
+        n2_list = load_list(n2, "n2_list")
+        load_scales(w1_scales_raw, w1_scales)
+        gain = keep.tile([P, SLABS], F32, name="gain")
+        nc.sync.dma_start(gain[:], gn.rearrange("(p t) o -> p (t o)", t=SLABS))
+        n1_list = load_list(n1, "n1_list")
+        w3_words_raw = load_weight_words(w3_words, "w3_words_raw")
+        load_scales(w3_scales_raw, w3_scales)
+        n3_list = load_list(n3, "n3_list")
+
+        def deal_words(raw, tag):
+            words = keep.tile([P, 2 * S], U8, name=tag, align_bytes=64)
+            nc.gpsimd.tensor_copy(
+                words[:].rearrange("p (t m e) -> p t m e", t=SLABS, e=2),
+                raw[:].rearrange("p (m t e) -> p t m e", t=SLABS, e=2),
             )
             return words
 
-        def deal_scales(scales_raw, name, tag):
-            scales = keep.tile([P, S], U8, name=name, tag=tag, align_bytes=64)
-            nc.vector.tensor_copy(
-                scales[:].rearrange("p (t m) -> p t m", t=PACK),
-                scales_raw[:].rearrange("p (m t) -> p t m", t=PACK),
+        def deal_scales(raw, tag):
+            scales = keep.tile([P, S], U8, name=tag, align_bytes=64)
+            nc.gpsimd.tensor_copy(
+                scales[:].rearrange("p (t m) -> p t m", t=SLABS),
+                raw[:].rearrange("p (m t) -> p t m", t=SLABS),
             )
             return scales
 
-        def pick_scales(lst, name, tag):
-            tile = keep.tile([P, S], U8, name=name, tag=tag, align_bytes=64)
-            nc.vector.tensor_copy(tile[:], xs[:].indirect(lst[:]))
+        def pick(table, places, dtype, name):
+            tile = keep.tile([P, S], dtype, name=name, align_bytes=64)
+            nc.vector.tensor_copy(tile[:], table[:].indirect(places[:]))
             return tile
 
-        def pick_words(lst, name, tag):
-            tile = keep.tile([P, S], U32, name=name, tag=tag, align_bytes=64)
-            nc.vector.tensor_copy(tile[:], xw[:].indirect(lst[:]))
-            return tile
-
-        def product(bank, weights, t, words, scales):
-            w_words, w_scales = weights
+        def product(out, weight, t, words, scales):
+            weight_words, weight_scales = weight
             nc.tensor.matmul_mx(
-                out=bank,
-                lhsT=w_words[:, 2 * P * t : 2 * P * (t + 1)].bitcast(FP4X4),
-                lhsT_scale=w_scales[:, P * t : P * (t + 1)],
+                out=out,
+                lhsT=weight_words[:, 2 * P * t : 2 * P * (t + 1)].bitcast(FP4X4),
+                lhsT_scale=weight_scales[:, P * t : P * (t + 1)],
                 rhs=words.bitcast(FP8X4),
                 rhs_scale=scales,
                 start=True,
                 stop=True,
             )
 
-        def gather_sub(out, window, lst, lo, hi, other):
-            nc.vector.tensor_tensor(out, window[:].indirect(lst[:, lo // 16 : hi // 16]), other, ALU.subtract)
+        def looked_up(window, places, lo, hi):
+            return window[:].indirect(places[:, lo // GROUP : hi // GROUP])
 
-        w2w = deal_words(w2w_raw, "w2w", "w2w")
-        xs_two = pick_scales(two_t, "xs_two", "xs_two")
-        xs_off = pick_scales(offs_t, "xs_off", "xs_off")
-        xw_two = pick_words(two_t, "xw_two", "xw_two")
-        w2 = (w2w, deal_scales(w2s_raw, "w2s", "w2s"))
-        xw_off = pick_words(offs_t, "xw_off", "w2s_raw")
-        w1 = (deal_words(w1w_raw, "w1w", "xw"), deal_scales(w1s_raw, "w1s", "w1w_raw"))
+        def gather_less(out, window, places, lo, hi, plain):
+            nc.vector.tensor_tensor(out, looked_up(window, places, lo, hi), plain, ALU.subtract)
 
-        last = PACK - 1
-        pieces = [(0, 256), (256, 384), (384, 512)]
+        def turn(out, block, start, stop):
+            nc.tensor.matmul(out, block, ident[:], start=start, stop=stop, is_transpose=True)
 
-        def by_four(ap):
-            return ap.rearrange("p t (c i) -> p c t i", i=4)
+        def slab_view(slabs):
+            return slabs.rearrange("p t (c i) -> p c t i", i=4)
 
-        def woven(tile):
-            return tile[:].rearrange("p (c i t) -> p c t i", i=4, t=PACK)
+        def woven_view(tile):
+            return tile[:].rearrange("p (c i t) -> p c t i", i=4, t=SLABS)
 
-        halves = [(0, 256), (256, 512)]
-        d_bank = [psum.tile([P, S], F32, name="bank%d" % t) for t in range(PACK)]
-        y_bank = [psum.tile([P, S], F32, name="bank%d" % (PACK + t)) for t in range(PACK)]
-        d_win = [keep.tile([P, S], F32, name="d_win%d" % t) for t in range(PACK)]
-        y_win = [keep.tile([P, S], F32, name="y_win%d" % t) for t in range(PACK)]
-        h_win = [keep.tile([P, 2 * S], F32, name="h_win%d" % t) for t in range(PACK)]
-        m_win = [keep.tile([P, 2 * S if t < last else S], F32, name="m_win%d" % t) for t in range(PACK)]
-        gate_last = keep.tile([P, S], F32, name="gate_last")
-        u = [h_win[t][:, S:] for t in range(PACK)]
-        gate_t = [m_win[t][:, S:] for t in range(last)] + [gate_last[:]]
-        y_own = keep.tile([P, PACK, S], F32, name="y_own")
-        v = keep.tile([P, PACK, S], F32, name="v")
-        pull = keep.tile([P, PACK, S], F32, name="pull")
+        w2_dealt_words = deal_words(w2_words_raw, "dealt_words_a")
+        two_scales = pick(x_scale_table, two_list, U8, "two_scales")
+        offs_scales = pick(x_scale_table, offs_list, U8, "offs_scales")
+        two_words = pick(x_word_table, two_list, U32, "two_words")
+        w2 = (w2_dealt_words, deal_scales(w2_scales_raw, "dealt_scales_a"))
+        offs_words = pick(x_word_table, offs_list, U32, "offs_words")
+        w1 = (deal_words(w1_words_raw, "dealt_words_b"), deal_scales(w1_scales_raw, "dealt_scales_b"))
 
-        for t in range(PACK):
-            product(d_bank[t][:], w2, t, xw_two[:], xs_two[:])
-        w3 = (deal_words(w3w_raw, "w3w", "w2w"), deal_scales(w3s_raw, "w3s", "w2s"))
-        for t in range(PACK):
-            product(y_bank[t][:], w1, t, xw_off[:], xs_off[:])
-        for t in range(PACK):
-            nc.scalar.copy(d_win[t][:], d_bank[t][:])
-        for t in range(PACK):
-            for lo, hi in halves:
-                picked = d_win[t][:].indirect(n2_t[:, lo // 16 : hi // 16])
-                nc.vector.tensor_scalar(u[t][:, lo:hi], picked, -1.0, 0.0, ALU.mult, ALU.add)
-        for t in range(PACK):
-            nc.scalar.activation(y_win[t][:], y_bank[t][:], ACT.Copy, scale=gain[:, t : t + 1])
-            nc.scalar.activation(y_own[:, t, :], y_bank[t][:], ACT.Copy, scale=gain[:, t : t + 1])
+        d_bank = [bank(t, [P, S]) for t in range(SLABS)]
+        y_bank = [bank(SLABS + t, [P, S]) for t in range(SLABS)]
+        d_window = [keep.tile([P, S], F32, name="d_window%d" % t) for t in range(SLABS)]
+        y_window = [keep.tile([P, S], F32, name="y_window%d" % t) for t in range(SLABS)]
+        h_window = [keep.tile([P, 2 * S], F32, name="h_window%d" % t) for t in range(SLABS)]
+        st_window = [keep.tile([P, 2 * S if t < last else S], F32, name="st_window%d" % t) for t in range(SLABS)]
+        gate_turned_last = keep.tile([P, S], F32, name="gate_turned_last")
+        d_far_negated = [h_window[t][:, S:] for t in range(SLABS)]
+        gate_turned = [st_window[t][:, S:] for t in range(last)] + [gate_turned_last[:]]
+        y_plain = keep.tile([P, SLABS, S], F32, name="y_plain")
+        y_step = keep.tile([P, SLABS, S], F32, name="y_step")
+        pull = keep.tile([P, SLABS, S], F32, name="pull")
 
-        def turn(out, term, start, stop):
-            nc.tensor.matmul(out, term, ident[:], start=start, stop=stop, is_transpose=True)
+        for t in range(SLABS):
+            product(d_bank[t][:], w2, t, two_words[:], two_scales[:])
+        w3 = (deal_words(w3_words_raw, "dealt_words_a"), deal_scales(w3_scales_raw, "dealt_scales_a"))
+        for t in range(SLABS):
+            product(y_bank[t][:], w1, t, offs_words[:], offs_scales[:])
+
+        for t in range(SLABS):
+            nc.scalar.copy(d_window[t][:], d_bank[t][:])
+        for t in range(SLABS):
+            for lo, hi in HALVES:
+                far = looked_up(d_window[t], n2_list, lo, hi)
+                nc.vector.tensor_scalar(d_far_negated[t][:, lo:hi], far, -1.0, 0.0, ALU.mult, ALU.add)
+
+        for t in range(SLABS):
+            nc.scalar.activation(y_window[t][:], y_bank[t][:], ACT.Copy, scale=gain[:, t : t + 1])
+            nc.scalar.activation(y_plain[:, t, :], y_bank[t][:], ACT.Copy, scale=gain[:, t : t + 1])
 
         blocks = [slice(b * P, (b + 1) * P) for b in range(S // P)]
-        for t in range(PACK):
-            diff = psum.tile([P, S], F32, name="bank%d" % t)
+        for t in range(SLABS):
+            d_gap = bank(t, [P, S])
             for b, cols in enumerate(blocks):
-                turn(diff[:, cols], d_win[t][:, cols], b == 0, False)
+                turn(d_gap[:, cols], d_window[t][:, cols], b == 0, False)
             for b, cols in enumerate(blocks):
-                turn(diff[:, cols], u[t][:, cols], False, b == len(blocks) - 1)
-            nc.scalar.activation(gate_t[t], diff[:], ACT.Sigmoid, scale=-1.0)
+                turn(d_gap[:, cols], d_far_negated[t][:, cols], False, b == len(blocks) - 1)
+            nc.scalar.activation(gate_turned[t], d_gap[:], ACT.Sigmoid, scale=-1.0)
         gate = {}
-        for h in range(2):
-            for j in range(2):
-                gate[h, j] = psum.tile([P, 2, 256], F32, name="bank%d" % (PACK + 2 * j + h))
-        for t in range(PACK):
+        for half in range(2):
+            for pair in range(2):
+                gate[half, pair] = bank(SLABS + 2 * pair + half, [P, 2, S // 2])
+        for t in range(SLABS):
             for b, cols in enumerate(blocks):
-                turn(gate[b // 2, t // 2][:, t % 2, blocks[b % 2]], gate_t[t][:, cols], True, True)
+                turn(gate[b // 2, t // 2][:, t % 2, blocks[b % 2]], gate_turned[t][:, cols], True, True)
 
         z_words = keep.tile([P, S], U32, name="z_words", align_bytes=64)
         z_scales = keep.tile([P, S], U8, name="z_scales", align_bytes=64)
-        h_own = keep.tile([P, PACK, S], F32, name="h_own")
-        groups = [((0, 2), (2, 4)), ((0, 4),), ((0, 1), (1, 4))]
+        h_plain = keep.tile([P, SLABS, S], F32, name="h_plain")
         h_parts = []
-        for h, (a, b) in enumerate(halves):
-            for t in range(PACK):
-                gather_sub(v[:, t, a:b], y_win[t], n1_t, a, b, y_own[:, t, a:b])
-            for j in range(2):
-                pair = slice(2 * j, 2 * j + 2)
-                nc.vector.tensor_tensor(pull[:, pair, a:b], gate[h, j][:], v[:, pair, a:b], ALU.mult)
-            for (lo, hi), spans in zip(pieces, groups):
-                if a <= lo < b:
-                    z_bf = keep.tile([P, PACK * (hi - lo)], BF16, name="z_bf%d" % lo, align_bytes=64)
-                    nc.vector.tensor_tensor(woven(z_bf), by_four(pull[:, :, lo:hi]), by_four(y_own[:, :, lo:hi]), ALU.add)
-                    nc.vector.quantize_mx(out=z_words[:, lo:hi].bitcast(FP8X4), scales=z_scales[:, lo:hi], in_=z_bf[:])
-                    for t0, t1 in spans:
-                        bank = psum.tile([P, t1 - t0, hi - lo], F32, name="bank%d" % len(h_parts))
+        for half, (half_lo, half_hi) in enumerate(HALVES):
+            half_cols = slice(half_lo, half_hi)
+            for t in range(SLABS):
+                gather_less(y_step[:, t, half_cols], y_window[t], n1_list, half_lo, half_hi, y_plain[:, t, half_cols])
+            for pair in range(2):
+                slabs = slice(2 * pair, 2 * pair + 2)
+                nc.vector.tensor_tensor(pull[:, slabs, half_cols], gate[half, pair][:], y_step[:, slabs, half_cols], ALU.mult)
+            for (lo, hi), bank_slabs in zip(PIECES, H_BANK_SLABS):
+                if half_lo <= lo < half_hi:
+                    z_woven = keep.tile([P, SLABS * (hi - lo)], BF16, name="z_woven%d" % lo, align_bytes=64)
+                    nc.vector.tensor_tensor(
+                        woven_view(z_woven), slab_view(pull[:, :, lo:hi]), slab_view(y_plain[:, :, lo:hi]), ALU.add
+                    )
+                    nc.vector.quantize_mx(out=z_words[:, lo:hi].bitcast(FP8X4), scales=z_scales[:, lo:hi], in_=z_woven[:])
+                    for t0, t1 in bank_slabs:
+                        h_bank = bank(len(h_parts), [P, t1 - t0, hi - lo])
                         for t in range(t0, t1):
-                            product(bank[:, t - t0, :], w3, t, z_words[:, lo:hi], z_scales[:, lo:hi])
-                        h_parts.append((bank, t0, t1, lo, hi))
-        for t in range(PACK):
-            for bank, t0, t1, lo, hi in h_parts:
+                            product(h_bank[:, t - t0, :], w3, t, z_words[:, lo:hi], z_scales[:, lo:hi])
+                        h_parts.append((h_bank, t0, t1, lo, hi))
+
+        for t in range(SLABS):
+            for h_bank, t0, t1, lo, hi in h_parts:
                 if t0 <= t < t1:
-                    nc.scalar.activation(h_win[t][:, lo:hi], bank[:, t - t0, :], ACT.Copy, scale=0.5)
-            for bank, t0, t1, lo, hi in h_parts:
+                    nc.scalar.activation(h_window[t][:, lo:hi], h_bank[:, t - t0, :], ACT.Copy, scale=0.5)
+            for h_bank, t0, t1, lo, hi in h_parts:
                 if t0 == t:
-                    nc.scalar.activation(h_own[:, t0:t1, lo:hi], bank[:], ACT.Copy, scale=0.5)
+                    nc.scalar.activation(h_plain[:, t0:t1, lo:hi], h_bank[:], ACT.Copy, scale=0.5)
 
-        m_own = keep.tile([P, PACK, S], F32, name="m_own")
-        for t in range(PACK):
-            for lo, hi in ((0, 256), (256, 512)) if t == 0 else ((0, 512),):
-                gather_sub(m_win[t][:, lo:hi], h_win[t], n3_t, lo, hi, h_own[:, t, lo:hi])
-            nc.scalar.activation(m_own[:, t, :], m_win[t][:, :S], ACT.Copy, scale=2.0)
+        st_negated = keep.tile([P, SLABS, S], F32, name="st_negated")
+        for t in range(SLABS):
+            for lo, hi in HALVES if t == 0 else ((0, S),):
+                gather_less(st_window[t][:, lo:hi], h_window[t], n3_list, lo, hi, h_plain[:, t, lo:hi])
+            nc.scalar.activation(st_negated[:, t, :], st_window[t][:, :S], ACT.Copy, scale=2.0)
 
-        o_words = keep.tile([P, S], U32, name="o_words", align_bytes=64)
-        o_scales = keep.tile([P, S], U8, name="o_scales", align_bytes=64)
-        out_rows = out_0.rearrange("(p t) s -> p t s", t=PACK)
-        out_words = out_1[0].rearrange("p c r -> p (c r)").bitcast(I32)
-        res = keep.tile([P, PACK, S], F32, name="res")
+        out_words = keep.tile([P, S], U32, name="out_words", align_bytes=64)
+        out_scales = keep.tile([P, S], U8, name="out_scales", align_bytes=64)
+        out_0_slabs = out_0.rearrange("(p t) s -> p t s", t=SLABS)
+        out_1_words = out_1[0].rearrange("p c r -> p (c r)").bitcast(I32)
+        result = keep.tile([P, SLABS, S], F32, name="result")
         for t in range(last):
-            gather_sub(res[:, t, :], m_win[t], n3_t, 0, S, m_own[:, t, :])
-            nc.sync.dma_start(out_rows[:, t, :], res[:, t, :])
-        for lo, hi in pieces:
-            gather_sub(res[:, last, lo:hi], m_win[last], n3_t, lo, hi, m_own[:, last, lo:hi])
-        nc.sync.dma_start(out_rows[:, last, :], res[:, last, :])
-        o_bf = [keep.tile([P, PACK * (hi - lo)], BF16, name="o_bf%d" % lo, align_bytes=64) for lo, hi in pieces]
-        for i, (lo, hi) in enumerate(pieces):
-            if i == 0:
-                nc.scalar.copy(woven(o_bf[i]), by_four(res[:, :, lo:hi]))
-            else:
-                nc.vector.tensor_copy(woven(o_bf[i]), by_four(res[:, :, lo:hi]))
-        for i in (1, 2, 0):
-            lo, hi = pieces[i]
-            nc.vector.quantize_mx(out=o_words[:, lo:hi].bitcast(FP8X4), scales=o_scales[:, lo:hi], in_=o_bf[i][:])
-        for lo, hi in ((256, 512), (0, 256)):
-            nc.sync.dma_start(out_words[:, lo:hi], o_words[:, lo:hi].bitcast(I32))
+            gather_less(result[:, t, :], st_window[t], n3_list, 0, S, st_negated[:, t, :])
+            nc.sync.dma_start(out_0_slabs[:, t, :], result[:, t, :])
+        for lo, hi in PIECES:
+            gather_less(result[:, last, lo:hi], st_window[last], n3_list, lo, hi, st_negated[:, last, lo:hi])
+        nc.sync.dma_start(out_0_slabs[:, last, :], result[:, last, :])
+
+        result_woven = [
+            keep.tile([P, SLABS * (hi - lo)], BF16, name="result_woven%d" % lo, align_bytes=64) for lo, hi in PIECES
+        ]
+        for piece, (lo, hi) in enumerate(PIECES):
+            weave = nc.scalar.copy if piece == 0 else nc.vector.tensor_copy
+            weave(woven_view(result_woven[piece]), slab_view(result[:, :, lo:hi]))
+        for piece in (1, 2, 0):
+            lo, hi = PIECES[piece]
+            nc.vector.quantize_mx(
+                out=out_words[:, lo:hi].bitcast(FP8X4), scales=out_scales[:, lo:hi], in_=result_woven[piece][:]
+            )
+        for lo, hi in reversed(HALVES):
+            nc.sync.dma_start(out_1_words[:, lo:hi], out_words[:, lo:hi].bitcast(I32))
         for q in range(4):
             queue = nc.scalar if q % 2 else nc.sync
-            queue.dma_start(out_2[0, 4 * q : 4 * q + 4, :].bitcast(I32), o_scales[32 * q : 32 * q + 4, :].bitcast(I32))
+            queue.dma_start(out_2[0, 4 * q : 4 * q + 4, :].bitcast(I32), out_scales[32 * q : 32 * q + 4, :].bitcast(I32))

from contextlib import ExitStack

import concourse.mybir as mybir
from concourse.masks import make_identity

F32 = mybir.dt.float32
BF16 = mybir.dt.bfloat16
I32 = mybir.dt.int32
U32 = mybir.dt.uint32
U16 = mybir.dt.uint16
U8 = mybir.dt.uint8
FP8X4 = mybir.dt.float8_e4m3fn_x4
FP4X4 = mybir.dt.float4_e2m1fn_x4
ALU = mybir.AluOpType
ACT = mybir.ActivationFunctionType

P = 128
SLABS = 4
T = 2048
S = 512
GROUP = 16
FLOPS = 3 * 2 * S * S * S

HALVES = ((0, S // 2), (S // 2, S))
PIECES = ((0, S // 2), (S // 2, 3 * S // 4), (3 * S // 4, S))
H_BANK_SLABS = (((0, 2), (2, 4)), ((0, 4),), ((0, 1), (1, 4)))


def tile_picked_twlpullbtwice_none_po_kernel(
    tc, x_words, x_scales, w1_words, w1_scales, w2_words, w2_scales, gn, w3_words, w3_scales,
    offs, two, n1, n2, n3, out_0, out_1, out_2,
):
    nc = tc.nc
    last = SLABS - 1
    with ExitStack() as ctx:
        keep = ctx.enter_context(tc.tile_pool(name="keep", bufs=1))
        psum = ctx.enter_context(tc.psum_pool(name="psum", bufs=1))

        def bank(number, shape):
            return psum.tile(shape, F32, name="bank%d" % number)

        def scale_tile(width, name):
            tile = keep.tile([P, width], U8, name=name, align_bytes=64)
            nc.vector.memset(tile[:].bitcast(I32), 0)
            return tile

        def load_scales(tile, src):
            for q in range(4):
                nc.sync.dma_start(tile[32 * q : 32 * q + 4, :].bitcast(I32), src[0, 4 * q : 4 * q + 4, :].bitcast(I32))

        def load_list(src, name):
            tile = keep.tile([P, S // GROUP], U16, name=name)
            nc.sync.dma_start(tile[:], src)
            return tile

        def load_weight_words(src, name):
            tile = keep.tile([P, 2 * S], U8, name=name, align_bytes=64)
            nc.sync.dma_start(tile[:].bitcast(I32), src[0].bitcast(I32))
            return tile

        x_scale_table = scale_tile(T, "x_scale_table")
        w2_scales_raw = scale_tile(S, "w2_scales_raw")
        w1_scales_raw = scale_tile(S, "w1_scales_raw")
        w3_scales_raw = scale_tile(S, "w3_scales_raw")
        ident = keep.tile([P, P], F32, name="ident")
        nc.vector.memset(ident[:], 0.0)
        make_identity(nc, ident[:], nomemset=True)

        w2_words_raw = load_weight_words(w2_words, "w2_words_raw")
        two_list = load_list(two, "two_list")
        offs_list = load_list(offs, "offs_list")
        load_scales(x_scale_table, x_scales)
        x_word_table = keep.tile([P, T], U32, name="x_word_table", align_bytes=64)
        nc.sync.dma_start(x_word_table[:].bitcast(I32), x_words[0].rearrange("p c r -> p (c r)").bitcast(I32))
        load_scales(w2_scales_raw, w2_scales)
        w1_words_raw = load_weight_words(w1_words, "w1_words_raw")
        n2_list = load_list(n2, "n2_list")
        load_scales(w1_scales_raw, w1_scales)
        gain = keep.tile([P, SLABS], F32, name="gain")
        nc.sync.dma_start(gain[:], gn.rearrange("(p t) o -> p (t o)", t=SLABS))
        n1_list = load_list(n1, "n1_list")
        w3_words_raw = load_weight_words(w3_words, "w3_words_raw")
        load_scales(w3_scales_raw, w3_scales)
        n3_list = load_list(n3, "n3_list")

        def deal_words(raw, tag):
            words = keep.tile([P, 2 * S], U8, name=tag, align_bytes=64)
            nc.gpsimd.tensor_copy(
                words[:].rearrange("p (t m e) -> p t m e", t=SLABS, e=2),
                raw[:].rearrange("p (m t e) -> p t m e", t=SLABS, e=2),
            )
            return words

        def deal_scales(raw, tag):
            scales = keep.tile([P, S], U8, name=tag, align_bytes=64)
            nc.gpsimd.tensor_copy(
                scales[:].rearrange("p (t m) -> p t m", t=SLABS),
                raw[:].rearrange("p (m t) -> p t m", t=SLABS),
            )
            return scales

        def pick(table, places, dtype, name):
            tile = keep.tile([P, S], dtype, name=name, align_bytes=64)
            nc.vector.tensor_copy(tile[:], table[:].indirect(places[:]))
            return tile

        def product(out, weight, t, words, scales):
            weight_words, weight_scales = weight
            nc.tensor.matmul_mx(
                out=out,
                lhsT=weight_words[:, 2 * P * t : 2 * P * (t + 1)].bitcast(FP4X4),
                lhsT_scale=weight_scales[:, P * t : P * (t + 1)],
                rhs=words.bitcast(FP8X4),
                rhs_scale=scales,
                start=True,
                stop=True,
            )

        def looked_up(window, places, lo, hi):
            return window[:].indirect(places[:, lo // GROUP : hi // GROUP])

        def gather_less(out, window, places, lo, hi, plain):
            nc.vector.tensor_tensor(out, looked_up(window, places, lo, hi), plain, ALU.subtract)

        def turn(out, block, start, stop):
            nc.tensor.matmul(out, block, ident[:], start=start, stop=stop, is_transpose=True)

        def slab_view(slabs):
            return slabs.rearrange("p t (c i) -> p c t i", i=4)

        def woven_view(tile):
            return tile[:].rearrange("p (c i t) -> p c t i", i=4, t=SLABS)

        w2_dealt_words = deal_words(w2_words_raw, "dealt_words_a")
        two_scales = pick(x_scale_table, two_list, U8, "two_scales")
        offs_scales = pick(x_scale_table, offs_list, U8, "offs_scales")
        two_words = pick(x_word_table, two_list, U32, "two_words")
        w2 = (w2_dealt_words, deal_scales(w2_scales_raw, "dealt_scales_a"))
        offs_words = pick(x_word_table, offs_list, U32, "offs_words")
        w1 = (deal_words(w1_words_raw, "dealt_words_b"), deal_scales(w1_scales_raw, "dealt_scales_b"))

        d_bank = [bank(t, [P, S]) for t in range(SLABS)]
        y_bank = [bank(SLABS + t, [P, S]) for t in range(SLABS)]
        d_window = [keep.tile([P, S], F32, name="d_window%d" % t) for t in range(SLABS)]
        y_window = [keep.tile([P, S], F32, name="y_window%d" % t) for t in range(SLABS)]
        h_window = [keep.tile([P, 2 * S], F32, name="h_window%d" % t) for t in range(SLABS)]
        st_window = [keep.tile([P, 2 * S if t < last else S], F32, name="st_window%d" % t) for t in range(SLABS)]
        gate_turned_last = keep.tile([P, S], F32, name="gate_turned_last")
        d_far_negated = [h_window[t][:, S:] for t in range(SLABS)]
        gate_turned = [st_window[t][:, S:] for t in range(last)] + [gate_turned_last[:]]
        y_plain = keep.tile([P, SLABS, S], F32, name="y_plain")
        y_step = keep.tile([P, SLABS, S], F32, name="y_step")
        pull = keep.tile([P, SLABS, S], F32, name="pull")

        for t in range(SLABS):
            product(d_bank[t][:], w2, t, two_words[:], two_scales[:])
        w3 = (deal_words(w3_words_raw, "dealt_words_a"), deal_scales(w3_scales_raw, "dealt_scales_a"))
        for t in range(SLABS):
            product(y_bank[t][:], w1, t, offs_words[:], offs_scales[:])

        for t in range(SLABS):
            nc.scalar.copy(d_window[t][:], d_bank[t][:])
        for t in range(SLABS):
            for lo, hi in HALVES:
                far = looked_up(d_window[t], n2_list, lo, hi)
                nc.vector.tensor_scalar(d_far_negated[t][:, lo:hi], far, -1.0, 0.0, ALU.mult, ALU.add)

        for t in range(SLABS):
            nc.scalar.activation(y_window[t][:], y_bank[t][:], ACT.Copy, scale=gain[:, t : t + 1])
            nc.scalar.activation(y_plain[:, t, :], y_bank[t][:], ACT.Copy, scale=gain[:, t : t + 1])

        blocks = [slice(b * P, (b + 1) * P) for b in range(S // P)]
        for t in range(SLABS):
            d_gap = bank(t, [P, S])
            for b, cols in enumerate(blocks):
                turn(d_gap[:, cols], d_window[t][:, cols], b == 0, False)
            for b, cols in enumerate(blocks):
                turn(d_gap[:, cols], d_far_negated[t][:, cols], False, b == len(blocks) - 1)
            nc.scalar.activation(gate_turned[t], d_gap[:], ACT.Sigmoid, scale=-1.0)
        gate = {}
        for half in range(2):
            for pair in range(2):
                gate[half, pair] = bank(SLABS + 2 * pair + half, [P, 2, S // 2])
        for t in range(SLABS):
            for b, cols in enumerate(blocks):
                turn(gate[b // 2, t // 2][:, t % 2, blocks[b % 2]], gate_turned[t][:, cols], True, True)

        z_words = keep.tile([P, S], U32, name="z_words", align_bytes=64)
        z_scales = keep.tile([P, S], U8, name="z_scales", align_bytes=64)
        h_plain = keep.tile([P, SLABS, S], F32, name="h_plain")
        h_parts = []
        for half, (half_lo, half_hi) in enumerate(HALVES):
            half_cols = slice(half_lo, half_hi)
            for t in range(SLABS):
                gather_less(y_step[:, t, half_cols], y_window[t], n1_list, half_lo, half_hi, y_plain[:, t, half_cols])
            for pair in range(2):
                slabs = slice(2 * pair, 2 * pair + 2)
                nc.vector.tensor_tensor(pull[:, slabs, half_cols], gate[half, pair][:], y_step[:, slabs, half_cols], ALU.mult)
            for (lo, hi), bank_slabs in zip(PIECES, H_BANK_SLABS):
                if half_lo <= lo < half_hi:
                    z_woven = keep.tile([P, SLABS * (hi - lo)], BF16, name="z_woven%d" % lo, align_bytes=64)
                    nc.vector.tensor_tensor(
                        woven_view(z_woven), slab_view(pull[:, :, lo:hi]), slab_view(y_plain[:, :, lo:hi]), ALU.add
                    )
                    nc.vector.quantize_mx(out=z_words[:, lo:hi].bitcast(FP8X4), scales=z_scales[:, lo:hi], in_=z_woven[:])
                    for t0, t1 in bank_slabs:
                        h_bank = bank(len(h_parts), [P, t1 - t0, hi - lo])
                        for t in range(t0, t1):
                            product(h_bank[:, t - t0, :], w3, t, z_words[:, lo:hi], z_scales[:, lo:hi])
                        h_parts.append((h_bank, t0, t1, lo, hi))

        for t in range(SLABS):
            for h_bank, t0, t1, lo, hi in h_parts:
                if t0 <= t < t1:
                    nc.scalar.activation(h_window[t][:, lo:hi], h_bank[:, t - t0, :], ACT.Copy, scale=0.5)
            for h_bank, t0, t1, lo, hi in h_parts:
                if t0 == t:
                    nc.scalar.activation(h_plain[:, t0:t1, lo:hi], h_bank[:], ACT.Copy, scale=0.5)

        st_negated = keep.tile([P, SLABS, S], F32, name="st_negated")
        for t in range(SLABS):
            for lo, hi in HALVES if t == 0 else ((0, S),):
                gather_less(st_window[t][:, lo:hi], h_window[t], n3_list, lo, hi, h_plain[:, t, lo:hi])
            nc.scalar.activation(st_negated[:, t, :], st_window[t][:, :S], ACT.Copy, scale=2.0)

        out_words = keep.tile([P, S], U32, name="out_words", align_bytes=64)
        out_scales = keep.tile([P, S], U8, name="out_scales", align_bytes=64)
        out_0_slabs = out_0.rearrange("(p t) s -> p t s", t=SLABS)
        out_1_words = out_1[0].rearrange("p c r -> p (c r)").bitcast(I32)
        result = keep.tile([P, SLABS, S], F32, name="result")
        for t in range(last):
            gather_less(result[:, t, :], st_window[t], n3_list, 0, S, st_negated[:, t, :])
            nc.sync.dma_start(out_0_slabs[:, t, :], result[:, t, :])
        for lo, hi in PIECES:
            gather_less(result[:, last, lo:hi], st_window[last], n3_list, lo, hi, st_negated[:, last, lo:hi])
        nc.sync.dma_start(out_0_slabs[:, last, :], result[:, last, :])

        result_woven = [
            keep.tile([P, SLABS * (hi - lo)], BF16, name="result_woven%d" % lo, align_bytes=64) for lo, hi in PIECES
        ]
        for piece, (lo, hi) in enumerate(PIECES):
            weave = nc.scalar.copy if piece == 0 else nc.vector.tensor_copy
            weave(woven_view(result_woven[piece]), slab_view(result[:, :, lo:hi]))
        for piece in (1, 2, 0):
            lo, hi = PIECES[piece]
            nc.vector.quantize_mx(
                out=out_words[:, lo:hi].bitcast(FP8X4), scales=out_scales[:, lo:hi], in_=result_woven[piece][:]
            )
        for lo, hi in reversed(HALVES):
            nc.sync.dma_start(out_1_words[:, lo:hi], out_words[:, lo:hi].bitcast(I32))
        for q in range(4):
            queue = nc.scalar if q % 2 else nc.sync
            queue.dma_start(out_2[0, 4 * q : 4 * q + 4, :].bitcast(I32), out_scales[32 * q : 32 * q + 4, :].bitcast(I32))
